import numpy as np
import ml_dtypes


def mxq(x, axis, fmt="e4m3"):
    dtype, down = {"e4m3": (ml_dtypes.float8_e4m3fn, 7), "e5m2": (ml_dtypes.float8_e5m2, 14)}[fmt]
    v = np.moveaxis(np.asarray(x, np.float32).astype(ml_dtypes.bfloat16).astype(np.float64), axis, -1)
    blocks = v.reshape(v.shape[:-1] + (-1, 32))
    amax = np.abs(blocks).max(-1, keepdims=True)
    byte = np.maximum(np.where(amax > 0, np.frexp(amax)[1] - 1 + 127, 0) - down, 1)
    scale = np.exp2(byte - 127.0)
    codes = (blocks / scale).astype(np.float32).astype(dtype).astype(np.float64)
    return np.moveaxis((codes * scale).reshape(v.shape), -1, axis)


WIDE = False


def mx_kscale(k):
    if not WIDE:
        return np.ones(k)
    levels = np.array([10, -10, 5, -5, 0])
    if k % 512:
        return np.exp2(np.random.permutation(np.resize(levels, k // 32))).repeat(32)
    a = np.empty((k // 512, 16))
    for p in range(k // 512):
        a[p, :8] = np.random.permutation(np.resize(levels, 8))
        for g in range(8):
            far = levels[np.abs(levels - a[p, g]) >= 10]
            a[p, g + 8] = far[np.random.randint(len(far))]
    return np.exp2(a.ravel()).repeat(32)


def f64(x):
    return np.asarray(x).astype(np.float64)


def striped(idx):
    return np.tile(idx.reshape(-1, 16).T, (8, 1)).astype(np.uint16)


def unstriped(offs):
    return offs[:16].T.reshape(-1).astype(np.int64)


E2M1 = np.array([0.0, 0.5, 1.0, 1.5, 2.0, 3.0, 4.0, 6.0, -0.0, -0.5, -1.0, -1.5, -2.0, -3.0, -4.0, -6.0])


def pack_weight(w, fmt):
    k, n = w.shape
    w = f64(np.asarray(w, np.float32).astype(ml_dtypes.bfloat16)).reshape(k // 32, 32, n)
    amax = np.abs(w).max(1)
    if fmt == "e4m3":
        byte = np.frexp(amax)[1] - 1 + 127 - 7
    else:
        mant, ex = np.frexp(amax / 6.0)
        byte = np.where(mant > 0.5, ex, ex - 1) + 127
    byte = np.clip(np.where(amax > 0, byte, 1), 1, 254)
    scaled = (w * np.exp2(127.0 - byte)[:, None, :]).reshape(k, n).astype(np.float32)
    by_word = np.ascontiguousarray(scaled.reshape(k // 512, 128, 4, n).transpose(0, 1, 3, 2))
    if fmt == "e4m3":
        words = by_word.astype(ml_dtypes.float8_e4m3fn).view(np.uint8)
    else:
        c = by_word.astype(ml_dtypes.float4_e2m1fn).view(np.uint8) & 0xF
        words = (c[..., 0::2] | (c[..., 1::2] << 4)).reshape(k // 512, 128, 2 * n)
    return np.ascontiguousarray(words), np.ascontiguousarray(byte.astype(np.uint8).reshape(k // 512, 16, n))


def unpack_weight(words, scales, fmt):
    g, _, n = scales.shape
    words = np.ascontiguousarray(words).reshape(g, 128, n, -1)
    if fmt == "e4m3":
        vals = words.view(ml_dtypes.float8_e4m3fn).astype(np.float64)
    else:
        nib = np.empty((g, 128, n, 4), np.uint8)
        nib[..., 0::2] = words & 0xF
        nib[..., 1::2] = words >> 4
        vals = E2M1[nib]
    vals = vals * np.repeat(np.exp2(scales.astype(np.float64) - 127.0), 8, axis=1)[..., None]
    return vals.transpose(0, 1, 3, 2).reshape(g * 512, n)


def silu(v):
    return v / (1.0 + np.exp(-np.maximum(v, -700.0)))


K, T, E, C, N = 2048, 768, 12, 256, 128
TOP = 4


def by_expert(wq, xq):
    return np.concatenate([wq[e].T @ xq[:, e * C:(e + 1) * C] for e in range(E)], axis=1)


def setup_inputs():
    n = np.random.standard_normal
    s = mx_kscale(K)[:, None]
    deal = np.repeat(np.arange(E), C).reshape(TOP, T)[:, np.random.permutation(T)]
    deal = np.take_along_axis(deal, np.argsort(np.random.rand(TOP, T), axis=0), axis=0)
    for _ in range(8):
        s_, t_ = np.random.permutation(T).reshape(2, -1); r = np.random.randint(TOP, size=T // 2); x, y = deal[r, s_].copy(), deal[r, t_].copy()
        ok = ~((deal[:, s_] == y).any(0) | (deal[:, t_] == x).any(0)); deal[r[ok], s_[ok]] = y[ok]; deal[r[ok], t_[ok]] = x[ok]
    order = np.lexsort((np.random.rand(TOP * T), deal.reshape(-1)))
    slot_token = order % T; pos = np.empty(TOP * T, np.int64); pos[order] = np.arange(TOP * T); pos = pos.reshape(TOP, T)
    g = np.random.uniform(0.5, 1.5, (TOP, T)); g = g / g.sum(0)
    w = [pack_weight(m, "e2m1") for m in n((E + 1, K, N)) / np.sqrt(K) / s[None]]
    return {
        "xT": (n((K, T)) * s).astype(np.float32),
        "w_words": np.stack([m[0] for m in w]),
        "w_scales": np.stack([m[1] for m in w]),
        "b": (0.3 * n((N, E + 1))).astype(np.float32),
        "gate": np.stack([np.tile(r, (N, 1)) for r in g]).astype(np.float32),
        "offs": striped(slot_token),
        "pos1": striped(pos[0]),
        "pos2": striped(pos[1]),
        "pos3": striped(pos[2]),
        "pos4": striped(pos[3]),
    }


def reference(xT, w_words, w_scales, b, gate, offs, pos1, pos2, pos3, pos4):
    idx = unstriped(offs)
    w = np.stack([unpack_weight(w_words[e], w_scales[e], "e2m1") for e in range(E + 1)])
    wq = w
    xs = mxq(f64(xT), 0, "e4m3")
    ys = silu((wq[E].T @ xs) + f64(b)[:, E:])
    xq = mxq(f64(xT)[:, idx], 0, "e4m3")
    y = by_expert(w, xq)
    y = silu(y + np.repeat(f64(b)[:, :E], C, axis=1))
    return ys + sum(f64(gate[r]) * y[:, unstriped(p)] for r, p in enumerate((pos1, pos2, pos3, pos4)))

@@ -1,0 +1,239 @@
+from contextlib import ExitStack
+
+import concourse.mybir as mybir
+from concourse.masks import make_identity
+
+K, T, E, C, N = 2048, 768, 12, 256, 128
+TOP = 4
+S = E * C
+FLOPS = 2 * K * N * (S + T)
+
+F32 = mybir.dt.float32
+BF16 = mybir.dt.bfloat16
+I32 = mybir.dt.int32
+U32 = mybir.dt.uint32
+U16 = mybir.dt.uint16
+U8 = mybir.dt.uint8
+FP8X4 = mybir.dt.float8_e4m3fn_x4
+FP4X4 = mybir.dt.float4_e2m1fn_x4
+ACT = mybir.ActivationFunctionType
+ALU = mybir.AluOpType
+
+P = 128
+PASSES = K // 512
+HALF = T // 2
+BLOCKS = HALF // P
+
+
+def tile_moe_shr_lin_silu_kernel(tc, xT, w_words, w_scales, b, gate, offs, pos1, pos2, pos3, pos4, out):
+    nc = tc.nc
+    with ExitStack() as ctx:
+        lists = ctx.enter_context(tc.tile_pool(name="lists", bufs=1))
+        keep = ctx.enter_context(tc.tile_pool(name="keep", bufs=1))
+        raws = ctx.enter_context(tc.tile_pool(name="raws", bufs=4))
+        ring = ctx.enter_context(tc.tile_pool(name="ring", bufs=1))
+        tail = ctx.enter_context(tc.tile_pool(name="tail", bufs=4))
+        psum = ctx.enter_context(tc.psum_pool(name="psum", bufs=1))
+
+        offs_sb = lists.tile([P, S // 16], U16, name="offs_sb")
+        nc.sync.dma_start(offs_sb[:], offs)
+
+        raw = {}
+
+        def load_rows(a, u):
+            raw[a, u] = raws.tile([P, 2, T], F32, name="raw")
+            rows = xT[512 * a:512 * (a + 1), :].rearrange("(p u e) t -> p u e t", u=2, e=2)
+            nc.sync.dma_start(raw[a, u][:], rows[:, u, :, :])
+
+        for a in range(2):
+            for u in range(2):
+                load_rows(a, u)
+
+        planes = keep.tile([P, 2 * PASSES * T * 2], BF16, name="planes", align_bytes=64)
+
+        def plane_start(a, u):
+            return (2 * (PASSES - 1 - a) + u) * T
+
+        def cast(eng, a, u, t0, t1):
+            c0 = 2 * plane_start(a, u)
+            dst = planes[:, c0 + 2 * t0:c0 + 2 * t1].rearrange("p (t e) -> p t e", e=2)
+            src = raw[a, u][:, :, t0:t1].rearrange("p e t -> p t e")
+            if eng == "v":
+                nc.vector.tensor_copy(dst, src)
+            else:
+                nc.scalar.copy(dst, src)
+
+        w_scale_sb = keep.tile([P, (E + 1) * PASSES * N], U8, name="w_scale_sb", align_bytes=64)
+        nc.vector.memset(w_scale_sb[:].bitcast(I32), 0)
+        gate_rows = keep.tile([P, P], F32, name="gate_rows")
+        nc.vector.memset(gate_rows[:], 0.0)
+        ident = keep.tile([P, P], F32, name="ident")
+        make_identity(nc, ident[:])
+
+        cast("v", 0, 0, 0, 512)
+        cast("s", 0, 0, 512, T)
+        cast("s", 0, 1, 0, T)
+
+        for u in range(2):
+            load_rows(2, u)
+        w_sb = keep.tile([P, (E + 1) * PASSES * 2 * N], U8, name="w_sb", align_bytes=64)
+        w_dst = w_sb[:].bitcast(I32).rearrange("p (g c) -> p g c", c=2 * N // 4)
+        w_src = w_words.rearrange("e a p c -> p (e a) c").bitcast(I32)
+        for g0, g1 in ((0, 24), (24, 52)):
+            nc.sync.dma_start(w_dst[:, g0:g1, :], w_src[:, g0:g1, :])
+        for u in range(2):
+            load_rows(3, u)
+        s_src = w_scales.rearrange("e a q n -> q (e a) n").bitcast(I32)
+        for q in range(4):
+            s_dst = w_scale_sb[32 * q:32 * q + 4, :].bitcast(I32).rearrange("p (g c) -> p g c", c=N // 4)
+            nc.sync.dma_start(s_dst, s_src[4 * q:4 * q + 4, :, :])
+        bias = keep.tile([P, E + 1], F32, name="bias")
+        nc.sync.dma_start(bias[:], b)
+        pos_sb = []
+        for r, pos in enumerate((pos1, pos2, pos3, pos4)):
+            pos_sb.append(lists.tile([P, T // 16], U16, name="pos_sb%d" % r))
+            nc.sync.dma_start(pos_sb[r][:], pos)
+        for r in range(TOP):
+            nc.sync.dma_start(gate_rows[6 * r:6 * r + 6, :], gate[r, 0, :].rearrange("(j t) -> j t", t=P))
+
+        gate_ps = psum.tile([P, P], F32, name="gate_ps", tag="bank7")
+        nc.tensor.transpose(gate_ps[:], gate_rows[:], ident[:])
+        gate_cols = keep.tile([P, 32], F32, name="gate_cols")
+        nc.scalar.copy(gate_cols[:], gate_ps[:, 0:32])
+
+        codes = [keep.tile([P, S], U32, name="codes%d" % a, align_bytes=64) for a in range(PASSES)]
+        scales = [keep.tile([P, S + T], U8, name="scales%d" % a, align_bytes=64) for a in range(PASSES)]
+        shared_codes = [keep.tile([P, T], U32, name="shared_codes%d" % a, align_bytes=64) for a in range(PASSES - 1)]
+        y = keep.tile([P, S], F32, name="y")
+        ys = keep.tile([P, T], F32, name="ys")
+
+        steps = [(a, s0, 1024) for a in range(2) for s0 in range(0, S, 1024)]
+        for s0, n in ((0, 1024), (1024, 1024), (2048, 512), (2560, 256), (2816, 256)):
+            steps.extend([(2, s0, n), (3, s0, n)])
+
+        gathered = {}
+        woven = {}
+
+        def gather(i):
+            a, s0, n = steps[i]
+            gathered[i] = ring.tile([P, 2 * n], U32, name="gathered", tag="gathered%d" % (i % 2))
+            piece = min(n, 512 if a == 0 else 1024)
+            width = T if piece <= 512 else 2 * T
+            for u in range(2):
+                c0 = 2 * plane_start(a, u)
+                window = planes[:, c0:c0 + 2 * width].bitcast(U32)
+                for j in range(0, n, piece):
+                    idx = offs_sb[:, (s0 + j) // 16:(s0 + j + piece) // 16]
+                    nc.vector.tensor_copy(gathered[i][:, u * n + j:u * n + j + piece], window.indirect(idx))
+
+        def weave(i):
+            n = steps[i][2]
+            woven[i] = ring.tile([P, 4 * n], BF16, name="woven", tag="woven%d" % (i % 2), align_bytes=64)
+            nc.scalar.copy(woven[i][:].bitcast(U32).rearrange("p (n u) -> p n u", u=2),
+                           gathered[i][:].rearrange("p (u n) -> p n u", u=2))
+
+        def quantize(i):
+            a, s0, n = steps[i]
+            nc.vector.quantize_mx(out=codes[a][:, s0:s0 + n].bitcast(FP8X4), scales=scales[a][:, s0:s0 + n], in_=woven[i][:])
+
+        shared_woven = {}
+
+        def shared_weave(a):
+            shared_woven[a] = ring.tile([P, 4 * T], BF16, name="shared_woven", align_bytes=64)
+            c0 = 2 * plane_start(a, 0)
+            nc.scalar.copy(shared_woven[a][:].bitcast(U32).rearrange("p (t u) -> p t u", u=2),
+                           planes[:, c0:c0 + 4 * T].bitcast(U32).rearrange("p (u t) -> p t u", u=2))
+
+        def shared_quantize(a, t0, t1, dst):
+            nc.vector.quantize_mx(out=dst.bitcast(FP8X4), scales=scales[a][:, S + t0:S + t1], in_=shared_woven[a][:, 4 * t0:4 * t1])
+
+        def product(acc, e, a, rhs, rhs_scale):
+            g = e * PASSES + a
+            nc.tensor.matmul_mx(out=acc, lhsT=w_sb[:, g * 2 * N:(g + 1) * 2 * N].bitcast(FP4X4),
+                                lhsT_scale=w_scale_sb[:, g * N:(g + 1) * N],
+                                rhs=rhs.bitcast(FP8X4), rhs_scale=rhs_scale,
+                                start=(a == 0), stop=(a == PASSES - 1))
+
+        def expert(e):
+            acc = psum.tile([P, C], F32, name="acc", tag="bank%d" % (e % 4))
+            for h in range(2):
+                cols = slice(e * C + h * P, e * C + (h + 1) * P)
+                for a in range(PASSES):
+                    product(acc[:, h * P:(h + 1) * P], e, a, codes[a][:, cols], scales[a][:, cols])
+            nc.scalar.activation(y[:, e * C:(e + 1) * C], acc[:], ACT.Silu, bias=bias[:, e:e + 1])
+
+        def last_expert():
+            e = E - 1
+            accs = [psum.tile([P, P], F32, name="acc_last", tag="bank%d" % (6 + h)) for h in range(2)]
+            for a in range(PASSES):
+                for h in range(2):
+                    cols = slice(e * C + h * P, e * C + (h + 1) * P)
+                    product(accs[h][:], e, a, codes[a][:, cols], scales[a][:, cols])
+            for h in range(2):
+                nc.scalar.activation(y[:, e * C + h * P:e * C + (h + 1) * P], accs[h][:], ACT.Silu, bias=bias[:, e:e + 1])
+
+        def experts_after(i):
+            a, s0, n = steps[i]
+            if a == PASSES - 1:
+                for e in range(s0 // C, (s0 + n) // C):
+                    if e < E - 1:
+                        expert(e)
+                    else:
+                        last_expert()
+
+        last = len(steps) - 1
+        for i in range(len(steps)):
+            gather(i)
+            weave(i)
+            if i < 6:
+                cast("s", 1 + i // 2, i % 2, 0, T)
+            elif i < 10:
+                shared_weave(i - 6)
+            if i >= 1:
+                quantize(i - 1)
+                experts_after(i - 1)
+            if 7 <= i < 10:
+                shared_quantize(i - 7, 0, 512, shared_codes[i - 7][:, 0:512])
+                shared_quantize(i - 7, 512, T, shared_codes[i - 7][:, 512:T])
+        late_a = ring.tile([P, 512], U32, name="late_a", tag="woven%d" % ((last - 1) % 2), align_bytes=64)
+        shared_quantize(3, 0, 512, late_a[:])
+        quantize(last)
+        experts_after(last)
+        late_b = ring.tile([P, 256], U32, name="late_b", tag="woven%d" % (last % 2), align_bytes=64)
+        shared_quantize(3, 512, T, late_b[:])
+
+        acc_a = psum.tile([P, 512], F32, name="acc_a", tag="bank4")
+        for a in range(PASSES):
+            rhs = shared_codes[a][:, 0:512] if a < 3 else late_a[:]
+            product(acc_a[:], E, a, rhs, scales[a][:, S:S + 512])
+        acc_b = psum.tile([P, 256], F32, name="acc_b", tag="bank5")
+        for h in range(2):
+            for a in range(PASSES):
+                rhs = shared_codes[a][:, 512 + h * P:512 + (h + 1) * P] if a < 3 else late_b[:, h * P:(h + 1) * P]
+                product(acc_b[:, h * P:(h + 1) * P], E, a, rhs, scales[a][:, S + 512 + h * P:S + 512 + (h + 1) * P])
+        nc.scalar.activation(ys[:, 0:512], acc_a[:], ACT.Silu, bias=bias[:, E:E + 1])
+        nc.scalar.activation(ys[:, 512:T], acc_b[:], ACT.Silu, bias=bias[:, E:E + 1])
+
+        sum_banks = (2, 3, 6, 7, 4, 5)
+        for h in range(2):
+            sums = [psum.tile([P, P], F32, name="sums", tag="bank%d" % sum_banks[h * BLOCKS + j]) for j in range(BLOCKS)]
+            for r in range(TOP):
+                picked = tail.tile([P, HALF], F32, name="picked")
+                idx = pos_sb[r][:, h * HALF // 16:(h + 1) * HALF // 16]
+                nc.vector.tensor_copy(picked[:], y[:].indirect(idx))
+                turned = psum.tile([P, HALF], F32, name="turned", tag="bank%d" % (r % 2))
+                for j in range(BLOCKS):
+                    nc.tensor.transpose(turned[:, j * P:(j + 1) * P], picked[:, j * P:(j + 1) * P], ident[:])
+                gated = tail.tile([P, HALF], F32, name="gated")
+                for j in range(BLOCKS):
+                    col = 6 * r + h * BLOCKS + j
+                    nc.scalar.activation(gated[:, j * P:(j + 1) * P], turned[:, j * P:(j + 1) * P], ACT.Copy,
+                                         scale=gate_cols[:, col:col + 1])
+                for j in range(BLOCKS):
+                    nc.tensor.matmul(sums[j][:], gated[:, j * P:(j + 1) * P], ident[:], start=(r == 0), stop=(r == TOP - 1),
+                                     is_transpose=True)
+            result = tail.tile([P, HALF], F32, name="result")
+            for j in range(BLOCKS):
+                t0 = h * HALF + j * P
+                nc.vector.tensor_tensor(result[:, j * P:(j + 1) * P], sums[j][:], ys[:, t0:t0 + P], ALU.add)
+            nc.sync.dma_start(out[:, h * HALF:(h + 1) * HALF], result[:])

@@ -23,6 +23,8 @@ P = 128
 PASSES = K // 512
 HALF = T // 2
 BLOCKS = HALF // P
+SCALAR_FROM = 2048
+PIECE = 256
 
 
 def tile_moe_shr_lin_silu_kernel(tc, xT, w_words, w_scales, b, gate, offs, pos1, pos2, pos3, pos4, out):
@@ -35,9 +37,6 @@ def tile_moe_shr_lin_silu_kernel(tc, xT, w_words, w_scales, b, gate, offs, pos1,
         tail = ctx.enter_context(tc.tile_pool(name="tail", bufs=4))
         psum = ctx.enter_context(tc.psum_pool(name="psum", bufs=1))
 
-        offs_sb = lists.tile([P, S // 16], U16, name="offs_sb")
-        nc.sync.dma_start(offs_sb[:], offs)
-
         raw = {}
 
         def load_rows(a, u):
@@ -45,9 +44,12 @@ def tile_moe_shr_lin_silu_kernel(tc, xT, w_words, w_scales, b, gate, offs, pos1,
             rows = xT[512 * a:512 * (a + 1), :].rearrange("(p u e) t -> p u e t", u=2, e=2)
             nc.sync.dma_start(raw[a, u][:], rows[:, u, :, :])
 
-        for a in range(2):
-            for u in range(2):
-                load_rows(a, u)
+        load_rows(0, 0)
+        offs_sb = lists.tile([P, S // 16], U16, name="offs_sb")
+        nc.sync.dma_start(offs_sb[:], offs)
+        load_rows(0, 1)
+        load_rows(1, 0)
+        load_rows(1, 1)
 
         planes = keep.tile([P, 2 * PASSES * T * 2], BF16, name="planes", align_bytes=64)
 
@@ -70,6 +72,8 @@ def tile_moe_shr_lin_silu_kernel(tc, xT, w_words, w_scales, b, gate, offs, pos1,
         ident = keep.tile([P, P], F32, name="ident")
         make_identity(nc, ident[:])
 
+        warm = keep.tile([P, 1], F32, name="warm")
+        nc.scalar.activation(warm[:], gate_rows[:, 0:1], ACT.Silu)
         cast("v", 0, 0, 0, 512)
         cast("s", 0, 0, 512, T)
         cast("s", 0, 1, 0, T)
@@ -107,7 +111,7 @@ def tile_moe_shr_lin_silu_kernel(tc, xT, w_words, w_scales, b, gate, offs, pos1,
         y = keep.tile([P, S], F32, name="y")
         ys = keep.tile([P, T], F32, name="ys")
 
-        steps = [(a, s0, 1024) for a in range(2) for s0 in range(0, S, 1024)]
+        steps = [(0, s0, 1024) for s0 in range(0, SCALAR_FROM, 1024)] + [(1, s0, 1024) for s0 in range(0, S, 1024)]
         for s0, n in ((0, 1024), (1024, 1024), (2048, 512), (2560, 256), (2816, 256)):
             steps.extend([(2, s0, n), (3, s0, n)])
 
@@ -147,6 +151,27 @@ def tile_moe_shr_lin_silu_kernel(tc, xT, w_words, w_scales, b, gate, offs, pos1,
         def shared_quantize(a, t0, t1, dst):
             nc.vector.quantize_mx(out=dst.bitcast(FP8X4), scales=scales[a][:, S + t0:S + t1], in_=shared_woven[a][:, 4 * t0:4 * t1])
 
+        rows_bf = [keep.tile([P, T], BF16, name="rows_bf%d" % d) for d in range(4)]
+
+        def cast_rows():
+            for d in range(4):
+                nc.scalar.copy(rows_bf[d][:], raw[0, d // 2][:, d % 2, :])
+
+        scalar_woven = {}
+
+        def scalar_gather(j):
+            s0 = SCALAR_FROM + j * PIECE
+            staged = ring.tile([P, 4 * PIECE], BF16, name="staged", tag="staged%d" % (j % 2))
+            idx = offs_sb[:, s0 // 16:(s0 + PIECE) // 16]
+            for d in range(4):
+                nc.scalar.activation(staged[:, d * PIECE:(d + 1) * PIECE], rows_bf[d][:].indirect(idx), ACT.Copy)
+            scalar_woven[j] = ring.tile([P, 4 * PIECE], BF16, name="scalar_woven", tag="scalar_woven%d" % (j % 2), align_bytes=64)
+            nc.scalar.copy(scalar_woven[j][:].rearrange("p (n d) -> p n d", d=4), staged[:].rearrange("p (d n) -> p n d", d=4))
+
+        def scalar_quantize(j):
+            s0 = SCALAR_FROM + j * PIECE
+            nc.vector.quantize_mx(out=codes[0][:, s0:s0 + PIECE].bitcast(FP8X4), scales=scales[0][:, s0:s0 + PIECE], in_=scalar_woven[j][:])
+
         def product(acc, e, a, rhs, rhs_scale):
             g = e * PASSES + a
             nc.tensor.matmul_mx(out=acc, lhsT=w_sb[:, g * 2 * N:(g + 1) * 2 * N].bitcast(FP4X4),
@@ -154,67 +179,81 @@ def tile_moe_shr_lin_silu_kernel(tc, xT, w_words, w_scales, b, gate, offs, pos1,
                                 rhs=rhs.bitcast(FP8X4), rhs_scale=rhs_scale,
                                 start=(a == 0), stop=(a == PASSES - 1))
 
-        def expert(e):
-            acc = psum.tile([P, C], F32, name="acc", tag="bank%d" % (e % 4))
-            for h in range(2):
+        sums_of = {}
+
+        def expert_products(e):
+            if e < E - 1:
+                acc = psum.tile([P, C], F32, name="acc", tag="bank%d" % (e % 4))
+                sums_of[e] = [(acc[:], e * C, C)]
+                order = [(acc[:, h * P:(h + 1) * P], h, a) for h in range(2) for a in range(PASSES)]
+            else:
+                accs = [psum.tile([P, P], F32, name="acc_last", tag="bank%d" % (3 + 4 * h)) for h in range(2)]
+                sums_of[e] = [(accs[h][:], e * C + h * P, P) for h in range(2)]
+                order = [(accs[h][:], h, a) for a in range(PASSES) for h in range(2)]
+            for dst, h, a in order:
                 cols = slice(e * C + h * P, e * C + (h + 1) * P)
-                for a in range(PASSES):
-                    product(acc[:, h * P:(h + 1) * P], e, a, codes[a][:, cols], scales[a][:, cols])
-            nc.scalar.activation(y[:, e * C:(e + 1) * C], acc[:], ACT.Silu, bias=bias[:, e:e + 1])
+                product(dst, e, a, codes[a][:, cols], scales[a][:, cols])
 
-        def last_expert():
-            e = E - 1
-            accs = [psum.tile([P, P], F32, name="acc_last", tag="bank%d" % (6 + h)) for h in range(2)]
-            for a in range(PASSES):
-                for h in range(2):
-                    cols = slice(e * C + h * P, e * C + (h + 1) * P)
-                    product(accs[h][:], e, a, codes[a][:, cols], scales[a][:, cols])
-            for h in range(2):
-                nc.scalar.activation(y[:, e * C + h * P:e * C + (h + 1) * P], accs[h][:], ACT.Silu, bias=bias[:, e:e + 1])
+        def expert_silu(e):
+            for acc, c0, n in sums_of[e]:
+                nc.scalar.activation(y[:, c0:c0 + n], acc, ACT.Silu, bias=bias[:, e:e + 1])
 
-        def experts_after(i):
+        def experts_of(i):
             a, s0, n = steps[i]
-            if a == PASSES - 1:
-                for e in range(s0 // C, (s0 + n) // C):
-                    if e < E - 1:
-                        expert(e)
-                    else:
-                        last_expert()
+            return range(s0 // C, (s0 + n) // C) if a == PASSES - 1 else ()
+
+        def shared_quantize_whole(a):
+            shared_quantize(a, 0, 512, shared_codes[a][:, 0:512])
+            shared_quantize(a, 512, T, shared_codes[a][:, 512:T])
+
+        casts_at = {0: [(1, 1)], 2: [(2, 0), (2, 1)], 3: [(3, 0)], 4: [(3, 1)]}
+        pieces_at = {1: 0, 3: 1, 5: 2, 7: 3}
+        shared_at = {1: 0, 4: 1, 6: 2, 8: 3}
+        shared_groups = ((0, 512), (512, P), (512 + P, P))
+        shared_sums = [psum.tile([P, n], F32, name="shared_sums", tag="bank%d" % (4 + j)) for j, (t0, n) in enumerate(shared_groups)]
+
+        def shared_products(a, operands):
+            for j, (t0, n) in enumerate(shared_groups):
+                product(shared_sums[j][:], E, a, operands[j], scales[a][:, S + t0:S + t0 + n])
 
         last = len(steps) - 1
+        cast_rows()
+        cast("s", 1, 0, 0, T)
         for i in range(len(steps)):
             gather(i)
             weave(i)
-            if i < 6:
-                cast("s", 1 + i // 2, i % 2, 0, T)
-            elif i < 10:
-                shared_weave(i - 6)
+            if i - 1 in shared_at and shared_at[i - 1] < 3:
+                a = shared_at[i - 1]
+                shared_quantize_whole(a)
+                shared_products(a, [shared_codes[a][:, t0:t0 + n] for t0, n in shared_groups])
+            for a, u in casts_at.get(i, ()):
+                cast("s", a, u, 0, T)
+            if i in shared_at:
+                shared_weave(shared_at[i])
+            if i in pieces_at:
+                scalar_gather(pieces_at[i])
+            if i >= 2:
+                for e in experts_of(i - 2):
+                    expert_silu(e)
             if i >= 1:
                 quantize(i - 1)
-                experts_after(i - 1)
-            if 7 <= i < 10:
-                shared_quantize(i - 7, 0, 512, shared_codes[i - 7][:, 0:512])
-                shared_quantize(i - 7, 512, T, shared_codes[i - 7][:, 512:T])
+                for e in experts_of(i - 1):
+                    expert_products(e)
+            if i - 1 in pieces_at:
+                scalar_quantize(pieces_at[i - 1])
         late_a = ring.tile([P, 512], U32, name="late_a", tag="woven%d" % ((last - 1) % 2), align_bytes=64)
         shared_quantize(3, 0, 512, late_a[:])
         quantize(last)
-        experts_after(last)
+        for e in experts_of(last):
+            expert_products(e)
+            expert_silu(e)
         late_b = ring.tile([P, 256], U32, name="late_b", tag="woven%d" % (last % 2), align_bytes=64)
         shared_quantize(3, 512, T, late_b[:])
+        shared_products(3, [late_a[:], late_b[:, 0:P], late_b[:, P:2 * P]])
+        for j, (t0, n) in enumerate(shared_groups):
+            nc.scalar.activation(ys[:, t0:t0 + n], shared_sums[j][:], ACT.Silu, bias=bias[:, E:E + 1])
 
-        acc_a = psum.tile([P, 512], F32, name="acc_a", tag="bank4")
-        for a in range(PASSES):
-            rhs = shared_codes[a][:, 0:512] if a < 3 else late_a[:]
-            product(acc_a[:], E, a, rhs, scales[a][:, S:S + 512])
-        acc_b = psum.tile([P, 256], F32, name="acc_b", tag="bank5")
-        for h in range(2):
-            for a in range(PASSES):
-                rhs = shared_codes[a][:, 512 + h * P:512 + (h + 1) * P] if a < 3 else late_b[:, h * P:(h + 1) * P]
-                product(acc_b[:, h * P:(h + 1) * P], E, a, rhs, scales[a][:, S + 512 + h * P:S + 512 + (h + 1) * P])
-        nc.scalar.activation(ys[:, 0:512], acc_a[:], ACT.Silu, bias=bias[:, E:E + 1])
-        nc.scalar.activation(ys[:, 512:T], acc_b[:], ACT.Silu, bias=bias[:, E:E + 1])
-
-        sum_banks = (2, 3, 6, 7, 4, 5)
+        sum_banks = (2, 3, 7, 4, 5, 6)
         for h in range(2):
             sums = [psum.tile([P, P], F32, name="sums", tag="bank%d" % sum_banks[h * BLOCKS + j]) for j in range(BLOCKS)]
             for r in range(TOP):
@@ -236,4 +275,4 @@ def tile_moe_shr_lin_silu_kernel(tc, xT, w_words, w_scales, b, gate, offs, pos1,
             for j in range(BLOCKS):
                 t0 = h * HALF + j * P
                 nc.vector.tensor_tensor(result[:, j * P:(j + 1) * P], sums[j][:], ys[:, t0:t0 + P], ALU.add)
-            nc.sync.dma_start(out[:, h * HALF:(h + 1) * HALF], result[:])
+                nc.sync.dma_start(out[:, t0:t0 + P], result[:, j * P:(j + 1) * P])

@@ -23,8 +23,8 @@ P = 128
 PASSES = K // 512
 HALF = T // 2
 BLOCKS = HALF // P
-SCALAR_FROM = 2048
-PIECE = 256
+SCALAR_FROM = 1792
+PIECE = 512
 
 
 def tile_moe_shr_lin_silu_kernel(tc, xT, w_words, w_scales, b, gate, offs, pos1, pos2, pos3, pos4, out):
@@ -111,9 +111,9 @@ def tile_moe_shr_lin_silu_kernel(tc, xT, w_words, w_scales, b, gate, offs, pos1,
         y = keep.tile([P, S], F32, name="y")
         ys = keep.tile([P, T], F32, name="ys")
 
-        steps = [(0, s0, 1024) for s0 in range(0, SCALAR_FROM, 1024)] + [(1, s0, 1024) for s0 in range(0, S, 1024)]
-        for s0, n in ((0, 1024), (1024, 1024), (2048, 512), (2560, 256), (2816, 256)):
-            steps.extend([(2, s0, n), (3, s0, n)])
+        steps = [(0, 0, 768), (0, 768, 1024)] + [(1, s0, 1024) for s0 in range(0, S, 1024)]
+        steps += [(a, s0, 1024) for s0 in (0, 1024) for a in (2, 3)]
+        steps += [(2, 2048, 1024), (3, 2048, 512), (3, 2560, 256), (3, 2816, 256)]
 
         gathered = {}
         woven = {}
@@ -121,14 +121,15 @@ def tile_moe_shr_lin_silu_kernel(tc, xT, w_words, w_scales, b, gate, offs, pos1,
         def gather(i):
             a, s0, n = steps[i]
             gathered[i] = ring.tile([P, 2 * n], U32, name="gathered", tag="gathered%d" % (i % 2))
-            piece = min(n, 512 if a == 0 else 1024)
-            width = T if piece <= 512 else 2 * T
             for u in range(2):
+                piece = min(n, 512 if a == 0 or (i, u) == (2, 0) else 1024)
+                width = T if piece <= 512 else 2 * T
                 c0 = 2 * plane_start(a, u)
                 window = planes[:, c0:c0 + 2 * width].bitcast(U32)
                 for j in range(0, n, piece):
-                    idx = offs_sb[:, (s0 + j) // 16:(s0 + j + piece) // 16]
-                    nc.vector.tensor_copy(gathered[i][:, u * n + j:u * n + j + piece], window.indirect(idx))
+                    end = min(n, j + piece)
+                    idx = offs_sb[:, (s0 + j) // 16:(s0 + end) // 16]
+                    nc.vector.tensor_copy(gathered[i][:, u * n + j:u * n + end], window.indirect(idx))
 
         def weave(i):
             n = steps[i][2]
@@ -138,7 +139,9 @@ def tile_moe_shr_lin_silu_kernel(tc, xT, w_words, w_scales, b, gate, offs, pos1,
 
         def quantize(i):
             a, s0, n = steps[i]
-            nc.vector.quantize_mx(out=codes[a][:, s0:s0 + n].bitcast(FP8X4), scales=scales[a][:, s0:s0 + n], in_=woven[i][:])
+            for j0, j1 in ((0, 512), (512, n)) if n == 768 else ((0, n),):
+                nc.vector.quantize_mx(out=codes[a][:, s0 + j0:s0 + j1].bitcast(FP8X4), scales=scales[a][:, s0 + j0:s0 + j1],
+                                      in_=woven[i][:, 4 * j0:4 * j1])
 
         shared_woven = {}
 
@@ -151,26 +154,35 @@ def tile_moe_shr_lin_silu_kernel(tc, xT, w_words, w_scales, b, gate, offs, pos1,
         def shared_quantize(a, t0, t1, dst):
             nc.vector.quantize_mx(out=dst.bitcast(FP8X4), scales=scales[a][:, S + t0:S + t1], in_=shared_woven[a][:, 4 * t0:4 * t1])
 
-        rows_bf = [keep.tile([P, T], BF16, name="rows_bf%d" % d) for d in range(4)]
+        rows_bf = [keep.tile([P, 2 * PIECE], BF16, name="rows_bf%d" % d) for d in range(4)]
+        for d in range(4):
+            nc.vector.memset(rows_bf[d][:, T:], 0.0)
 
         def cast_rows():
             for d in range(4):
-                nc.scalar.copy(rows_bf[d][:], raw[0, d // 2][:, d % 2, :])
+                nc.scalar.copy(rows_bf[d][:, 0:T], raw[0, d // 2][:, d % 2, :])
 
         scalar_woven = {}
 
-        def scalar_gather(j):
-            s0 = SCALAR_FROM + j * PIECE
-            staged = ring.tile([P, 4 * PIECE], BF16, name="staged", tag="staged%d" % (j % 2))
-            idx = offs_sb[:, s0 // 16:(s0 + PIECE) // 16]
-            for d in range(4):
-                nc.scalar.activation(staged[:, d * PIECE:(d + 1) * PIECE], rows_bf[d][:].indirect(idx), ACT.Copy)
-            scalar_woven[j] = ring.tile([P, 4 * PIECE], BF16, name="scalar_woven", tag="scalar_woven%d" % (j % 2), align_bytes=64)
-            nc.scalar.copy(scalar_woven[j][:].rearrange("p (n d) -> p n d", d=4), staged[:].rearrange("p (d n) -> p n d", d=4))
+        staged = {}
+        pieces = [(s0, min(PIECE, S - s0)) for s0 in range(SCALAR_FROM, S, PIECE)]
+
+        def scalar_gather(j, rows):
+            s0, n = pieces[j]
+            if j not in staged:
+                staged[j] = ring.tile([P, 4 * n], BF16, name="staged", tag="staged%d" % (j % 2))
+            idx = offs_sb[:, s0 // 16:(s0 + n) // 16]
+            for d in rows:
+                nc.scalar.activation(staged[j][:, d * n:(d + 1) * n], rows_bf[d][:].indirect(idx), ACT.Copy)
+
+        def scalar_weave(j):
+            scalar_woven[j] = ring.tile([P, 4 * pieces[j][1]], BF16, name="scalar_woven", align_bytes=64)
+            nc.scalar.copy(scalar_woven[j][:].rearrange("p (c i d) -> p c d i", i=4, d=4),
+                           staged[j][:].rearrange("p (d c i) -> p c d i", d=4, i=4))
 
         def scalar_quantize(j):
-            s0 = SCALAR_FROM + j * PIECE
-            nc.vector.quantize_mx(out=codes[0][:, s0:s0 + PIECE].bitcast(FP8X4), scales=scales[0][:, s0:s0 + PIECE], in_=scalar_woven[j][:])
+            s0, n = pieces[j]
+            nc.vector.quantize_mx(out=codes[0][:, s0:s0 + n].bitcast(FP8X4), scales=scales[0][:, s0:s0 + n], in_=scalar_woven[j][:])
 
         def product(acc, e, a, rhs, rhs_scale):
             g = e * PASSES + a
@@ -206,9 +218,10 @@ def tile_moe_shr_lin_silu_kernel(tc, xT, w_words, w_scales, b, gate, offs, pos1,
             shared_quantize(a, 0, 512, shared_codes[a][:, 0:512])
             shared_quantize(a, 512, T, shared_codes[a][:, 512:T])
 
-        casts_at = {0: [(1, 1)], 2: [(2, 0), (2, 1)], 3: [(3, 0)], 4: [(3, 1)]}
-        pieces_at = {1: 0, 3: 1, 5: 2, 7: 3}
-        shared_at = {1: 0, 4: 1, 6: 2, 8: 3}
+        casts_at = {0: [(1, 0), (1, 1)], 2: [(2, 0), (2, 1)], 3: [(3, 0), (3, 1)]}
+        begun_at = {1: 0, 5: 1, 7: 2}
+        pieces_at = {4: 0, 6: 1, 8: 2}
+        shared_at = {1: 0, 4: 1, 7: 2, 9: 3}
         shared_groups = ((0, 512), (512, P), (512 + P, P))
         shared_sums = [psum.tile([P, n], F32, name="shared_sums", tag="bank%d" % (4 + j)) for j, (t0, n) in enumerate(shared_groups)]
 
@@ -217,8 +230,6 @@ def tile_moe_shr_lin_silu_kernel(tc, xT, w_words, w_scales, b, gate, offs, pos1,
                 product(shared_sums[j][:], E, a, operands[j], scales[a][:, S + t0:S + t0 + n])
 
         last = len(steps) - 1
-        cast_rows()
-        cast("s", 1, 0, 0, T)
         for i in range(len(steps)):
             gather(i)
             weave(i)
@@ -228,10 +239,15 @@ def tile_moe_shr_lin_silu_kernel(tc, xT, w_words, w_scales, b, gate, offs, pos1,
                 shared_products(a, [shared_codes[a][:, t0:t0 + n] for t0, n in shared_groups])
             for a, u in casts_at.get(i, ()):
                 cast("s", a, u, 0, T)
+            if i == 1:
+                cast_rows()
+            if i in pieces_at:
+                scalar_gather(pieces_at[i], (3,))
+                scalar_weave(pieces_at[i])
             if i in shared_at:
                 shared_weave(shared_at[i])
-            if i in pieces_at:
-                scalar_gather(pieces_at[i])
+            if i in begun_at:
+                scalar_gather(begun_at[i], (0, 1, 2))
             if i >= 2:
                 for e in experts_of(i - 2):
                     expert_silu(e)
@@ -243,6 +259,8 @@ def tile_moe_shr_lin_silu_kernel(tc, xT, w_words, w_scales, b, gate, offs, pos1,
                 scalar_quantize(pieces_at[i - 1])
         late_a = ring.tile([P, 512], U32, name="late_a", tag="woven%d" % ((last - 1) % 2), align_bytes=64)
         shared_quantize(3, 0, 512, late_a[:])
+        for e in experts_of(last - 1):
+            expert_silu(e)
         quantize(last)
         for e in experts_of(last):
             expert_products(e)

@@ -23,8 +23,9 @@ P = 128
 PASSES = K // 512
 HALF = T // 2
 BLOCKS = HALF // P
-SCALAR_FROM = 1792
+SCALAR_FROM = 1536
 PIECE = 512
+DIRECT = 2
 
 
 def tile_moe_shr_lin_silu_kernel(tc, xT, w_words, w_scales, b, gate, offs, pos1, pos2, pos3, pos4, out):
@@ -100,6 +101,10 @@ def tile_moe_shr_lin_silu_kernel(tc, xT, w_words, w_scales, b, gate, offs, pos1,
         for r in range(TOP):
             nc.sync.dma_start(gate_rows[6 * r:6 * r + 6, :], gate[r, 0, :].rearrange("(j t) -> j t", t=P))
 
+        gate_rest = {}
+        for r in range(TOP - DIRECT, TOP):
+            gate_rest[r] = keep.tile([P, HALF], F32, name="gate_rest%d" % r)
+            nc.sync.dma_start(gate_rest[r][:], gate[r, :, HALF:])
         gate_ps = psum.tile([P, P], F32, name="gate_ps", tag="bank7")
         nc.tensor.transpose(gate_ps[:], gate_rows[:], ident[:])
         gate_cols = keep.tile([P, 32], F32, name="gate_cols")
@@ -111,7 +116,7 @@ def tile_moe_shr_lin_silu_kernel(tc, xT, w_words, w_scales, b, gate, offs, pos1,
         y = keep.tile([P, S], F32, name="y")
         ys = keep.tile([P, T], F32, name="ys")
 
-        steps = [(0, 0, 768), (0, 768, 1024)] + [(1, s0, 1024) for s0 in range(0, S, 1024)]
+        steps = [(0, 0, 512), (0, 512, 1024)] + [(1, s0, 1024) for s0 in range(0, S, 1024)]
         steps += [(a, s0, 1024) for s0 in (0, 1024) for a in (2, 3)]
         steps += [(2, 2048, 1024), (3, 2048, 512), (3, 2560, 256), (3, 2816, 256)]
 
@@ -159,8 +164,9 @@ def tile_moe_shr_lin_silu_kernel(tc, xT, w_words, w_scales, b, gate, offs, pos1,
             nc.vector.memset(rows_bf[d][:, T:], 0.0)
 
         def cast_rows():
-            for d in range(4):
-                nc.scalar.copy(rows_bf[d][:, 0:T], raw[0, d // 2][:, d % 2, :])
+            for d in range(2):
+                nc.scalar.copy(rows_bf[d][:, 0:T], raw[0, 0][:, d, :])
+                nc.gpsimd.tensor_scalar(rows_bf[2 + d][:, 0:T], raw[0, 1][:, d, :], 1.0, 0.0, op0=ALU.mult, op1=ALU.add)
 
         scalar_woven = {}
 
@@ -218,10 +224,10 @@ def tile_moe_shr_lin_silu_kernel(tc, xT, w_words, w_scales, b, gate, offs, pos1,
             shared_quantize(a, 0, 512, shared_codes[a][:, 0:512])
             shared_quantize(a, 512, T, shared_codes[a][:, 512:T])
 
-        casts_at = {0: [(1, 0), (1, 1)], 2: [(2, 0), (2, 1)], 3: [(3, 0), (3, 1)]}
-        begun_at = {1: 0, 5: 1, 7: 2}
-        pieces_at = {4: 0, 6: 1, 8: 2}
-        shared_at = {1: 0, 4: 1, 7: 2, 9: 3}
+        casts_at = {0: [(1, 0), (1, 1)], 2: [(2, 0), (2, 1)], 3: [(3, 0)], 4: [(3, 1)]}
+        begun_at = {1: 0, 4: 1, 6: 2}
+        pieces_at = {3: 0, 5: 1, 7: 2}
+        shared_at = {1: 0, 5: 1, 7: 2, 9: 3}
         shared_groups = ((0, 512), (512, P), (512 + P, P))
         shared_sums = [psum.tile([P, n], F32, name="shared_sums", tag="bank%d" % (4 + j)) for j, (t0, n) in enumerate(shared_groups)]
 
@@ -273,8 +279,9 @@ def tile_moe_shr_lin_silu_kernel(tc, xT, w_words, w_scales, b, gate, offs, pos1,
 
         sum_banks = (2, 3, 7, 4, 5, 6)
         for h in range(2):
+            turned_terms = TOP - DIRECT * h
             sums = [psum.tile([P, P], F32, name="sums", tag="bank%d" % sum_banks[h * BLOCKS + j]) for j in range(BLOCKS)]
-            for r in range(TOP):
+            for r in range(turned_terms):
                 picked = tail.tile([P, HALF], F32, name="picked")
                 idx = pos_sb[r][:, h * HALF // 16:(h + 1) * HALF // 16]
                 nc.vector.tensor_copy(picked[:], y[:].indirect(idx))
@@ -287,10 +294,17 @@ def tile_moe_shr_lin_silu_kernel(tc, xT, w_words, w_scales, b, gate, offs, pos1,
                     nc.scalar.activation(gated[:, j * P:(j + 1) * P], turned[:, j * P:(j + 1) * P], ACT.Copy,
                                          scale=gate_cols[:, col:col + 1])
                 for j in range(BLOCKS):
-                    nc.tensor.matmul(sums[j][:], gated[:, j * P:(j + 1) * P], ident[:], start=(r == 0), stop=(r == TOP - 1),
+                    nc.tensor.matmul(sums[j][:], gated[:, j * P:(j + 1) * P], ident[:], start=(r == 0), stop=(r == turned_terms - 1),
                                      is_transpose=True)
-            result = tail.tile([P, HALF], F32, name="result")
+            rest = ys[:, h * HALF:(h + 1) * HALF]
+            for r in range(turned_terms, TOP):
+                direct = tail.tile([P, HALF], F32, name="picked")
+                nc.vector.tensor_tensor(direct[:], y[:].indirect(pos_sb[r][:, HALF // 16:]), gate_rest[r][:], ALU.mult)
+                added = tail.tile([P, HALF], F32, name="added", bufs=2)
+                nc.vector.tensor_tensor(added[:], direct[:], rest, ALU.add)
+                rest = added[:]
+            result = tail.tile([P, HALF], F32, name="result", bufs=2)
             for j in range(BLOCKS):
                 t0 = h * HALF + j * P
-                nc.vector.tensor_tensor(result[:, j * P:(j + 1) * P], sums[j][:], ys[:, t0:t0 + P], ALU.add)
+                nc.vector.tensor_tensor(result[:, j * P:(j + 1) * P], sums[j][:], rest[:, j * P:(j + 1) * P], ALU.add)
                 nc.sync.dma_start(out[:, t0:t0 + P], result[:, j * P:(j + 1) * P])

@@ -21,10 +21,14 @@ ALU = mybir.AluOpType
 
 P = 128
 PASSES = K // 512
+LONG = 1024
+NARROW = 512
+PIECE = 512
+SCALAR_FROM = LONG
+GPSIMD_FROM = 640
+FIRST_CAST_SPLIT = 512
 HALF = T // 2
 BLOCKS = HALF // P
-SCALAR_FROM = 1536
-PIECE = 512
 DIRECT = 2
 
 
@@ -35,7 +39,7 @@ def tile_moe_shr_lin_silu_kernel(tc, xT, w_words, w_scales, b, gate, offs, pos1,
         keep = ctx.enter_context(tc.tile_pool(name="keep", bufs=1))
         raws = ctx.enter_context(tc.tile_pool(name="raws", bufs=4))
         ring = ctx.enter_context(tc.tile_pool(name="ring", bufs=1))
-        tail = ctx.enter_context(tc.tile_pool(name="tail", bufs=4))
+        tail = ctx.enter_context(tc.tile_pool(name="tail", bufs=TOP))
         psum = ctx.enter_context(tc.psum_pool(name="psum", bufs=1))
 
         raw = {}
@@ -54,17 +58,13 @@ def tile_moe_shr_lin_silu_kernel(tc, xT, w_words, w_scales, b, gate, offs, pos1,
 
         planes = keep.tile([P, 2 * PASSES * T * 2], BF16, name="planes", align_bytes=64)
 
-        def plane_start(a, u):
-            return (2 * (PASSES - 1 - a) + u) * T
+        def plane_column(a, u):
+            return 2 * T * (2 * (PASSES - 1 - a) + u)
 
-        def cast(eng, a, u, t0, t1):
-            c0 = 2 * plane_start(a, u)
-            dst = planes[:, c0 + 2 * t0:c0 + 2 * t1].rearrange("p (t e) -> p t e", e=2)
-            src = raw[a, u][:, :, t0:t1].rearrange("p e t -> p t e")
-            if eng == "v":
-                nc.vector.tensor_copy(dst, src)
-            else:
-                nc.scalar.copy(dst, src)
+        def round_plane(copy, a, u, t0, t1):
+            c0 = plane_column(a, u)
+            copy(planes[:, c0 + 2 * t0:c0 + 2 * t1].rearrange("p (t e) -> p t e", e=2),
+                 raw[a, u][:, :, t0:t1].rearrange("p e t -> p t e"))
 
         w_scale_sb = keep.tile([P, (E + 1) * PASSES * N], U8, name="w_scale_sb", align_bytes=64)
         nc.vector.memset(w_scale_sb[:].bitcast(I32), 0)
@@ -75,40 +75,48 @@ def tile_moe_shr_lin_silu_kernel(tc, xT, w_words, w_scales, b, gate, offs, pos1,
 
         warm = keep.tile([P, 1], F32, name="warm")
         nc.scalar.activation(warm[:], gate_rows[:, 0:1], ACT.Silu)
-        cast("v", 0, 0, 0, 512)
-        cast("s", 0, 0, 512, T)
-        cast("s", 0, 1, 0, T)
+        round_plane(nc.vector.tensor_copy, 0, 0, 0, FIRST_CAST_SPLIT)
+        round_plane(nc.scalar.copy, 0, 0, FIRST_CAST_SPLIT, T)
+        round_plane(nc.scalar.copy, 0, 1, 0, T)
 
         for u in range(2):
             load_rows(2, u)
-        w_sb = keep.tile([P, (E + 1) * PASSES * 2 * N], U8, name="w_sb", align_bytes=64)
+        matrices = (E + 1) * PASSES
+        w_sb = keep.tile([P, matrices * 2 * N], U8, name="w_sb", align_bytes=64)
         w_dst = w_sb[:].bitcast(I32).rearrange("p (g c) -> p g c", c=2 * N // 4)
         w_src = w_words.rearrange("e a p c -> p (e a) c").bitcast(I32)
-        for g0, g1 in ((0, 24), (24, 52)):
+        first_six = 6 * PASSES
+        for g0, g1 in ((0, first_six), (first_six, matrices)):
             nc.sync.dma_start(w_dst[:, g0:g1, :], w_src[:, g0:g1, :])
         for u in range(2):
             load_rows(3, u)
         s_src = w_scales.rearrange("e a q n -> q (e a) n").bitcast(I32)
-        for q in range(4):
-            s_dst = w_scale_sb[32 * q:32 * q + 4, :].bitcast(I32).rearrange("p (g c) -> p g c", c=N // 4)
-            nc.sync.dma_start(s_dst, s_src[4 * q:4 * q + 4, :, :])
+        for quadrant in range(4):
+            s_dst = w_scale_sb[32 * quadrant:32 * quadrant + 4, :].bitcast(I32).rearrange("p (g c) -> p g c", c=N // 4)
+            nc.sync.dma_start(s_dst, s_src[4 * quadrant:4 * quadrant + 4, :, :])
         bias = keep.tile([P, E + 1], F32, name="bias")
         nc.sync.dma_start(bias[:], b)
         pos_sb = []
         for r, pos in enumerate((pos1, pos2, pos3, pos4)):
             pos_sb.append(lists.tile([P, T // 16], U16, name="pos_sb%d" % r))
             nc.sync.dma_start(pos_sb[r][:], pos)
-        for r in range(TOP):
-            nc.sync.dma_start(gate_rows[6 * r:6 * r + 6, :], gate[r, 0, :].rearrange("(j t) -> j t", t=P))
 
-        gate_rest = {}
+        gate_column = {}
+        gate_blocks = 0
+        for r in range(TOP):
+            blocks = 2 * BLOCKS if r < TOP - DIRECT else BLOCKS
+            nc.sync.dma_start(gate_rows[gate_blocks:gate_blocks + blocks, :],
+                              gate[r, 0, 0:blocks * P].rearrange("(j t) -> j t", t=P))
+            gate_column[r] = gate_blocks
+            gate_blocks = gate_blocks + blocks
+        gate_direct = {}
         for r in range(TOP - DIRECT, TOP):
-            gate_rest[r] = keep.tile([P, HALF], F32, name="gate_rest%d" % r)
-            nc.sync.dma_start(gate_rest[r][:], gate[r, :, HALF:])
+            gate_direct[r] = keep.tile([P, HALF], F32, name="gate_direct%d" % r)
+            nc.sync.dma_start(gate_direct[r][:], gate[r, :, HALF:])
         gate_ps = psum.tile([P, P], F32, name="gate_ps", tag="bank7")
         nc.tensor.transpose(gate_ps[:], gate_rows[:], ident[:])
-        gate_cols = keep.tile([P, 32], F32, name="gate_cols")
-        nc.scalar.copy(gate_cols[:], gate_ps[:, 0:32])
+        gate_cols = keep.tile([P, gate_blocks], F32, name="gate_cols")
+        nc.scalar.copy(gate_cols[:], gate_ps[:, 0:gate_blocks])
 
         codes = [keep.tile([P, S], U32, name="codes%d" % a, align_bytes=64) for a in range(PASSES)]
         scales = [keep.tile([P, S + T], U8, name="scales%d" % a, align_bytes=64) for a in range(PASSES)]
@@ -116,9 +124,11 @@ def tile_moe_shr_lin_silu_kernel(tc, xT, w_words, w_scales, b, gate, offs, pos1,
         y = keep.tile([P, S], F32, name="y")
         ys = keep.tile([P, T], F32, name="ys")
 
-        steps = [(0, 0, 512), (0, 512, 1024)] + [(1, s0, 1024) for s0 in range(0, S, 1024)]
-        steps += [(a, s0, 1024) for s0 in (0, 1024) for a in (2, 3)]
-        steps += [(2, 2048, 1024), (3, 2048, 512), (3, 2560, 256), (3, 2816, 256)]
+        steps = [(0, 0, SCALAR_FROM)] + [(1, s0, LONG) for s0 in range(0, S, LONG)]
+        steps += [(a, s0, LONG) for s0 in range(0, S - LONG, LONG) for a in (2, 3)]
+        steps += [(2, S - LONG, LONG), (3, S - LONG, 2 * C), (3, S - 2 * C, C), (3, S - C, C)]
+        last = len(steps) - 1
+        gpsimd_steps = [i for i in range(last) if steps[i + 1][2] == LONG]
 
         gathered = {}
         woven = {}
@@ -127,68 +137,66 @@ def tile_moe_shr_lin_silu_kernel(tc, xT, w_words, w_scales, b, gate, offs, pos1,
             a, s0, n = steps[i]
             gathered[i] = ring.tile([P, 2 * n], U32, name="gathered", tag="gathered%d" % (i % 2))
             for u in range(2):
-                piece = min(n, 512 if a == 0 or (i, u) == (2, 0) else 1024)
-                width = T if piece <= 512 else 2 * T
-                c0 = 2 * plane_start(a, u)
-                window = planes[:, c0:c0 + 2 * width].bitcast(U32)
-                for j in range(0, n, piece):
-                    end = min(n, j + piece)
-                    idx = offs_sb[:, (s0 + j) // 16:(s0 + end) // 16]
-                    nc.vector.tensor_copy(gathered[i][:, u * n + j:u * n + end], window.indirect(idx))
+                count = min(n, NARROW if a == 0 or (i, u) == (1, 0) else LONG)
+                words = T if count <= NARROW else 2 * T
+                c0 = plane_column(a, u)
+                window = planes[:, c0:c0 + 2 * words].bitcast(U32)
+                for j in range(0, n, count):
+                    idx = offs_sb[:, (s0 + j) // 16:(s0 + j + count) // 16]
+                    nc.vector.tensor_copy(gathered[i][:, u * n + j:u * n + j + count], window.indirect(idx))
+
+        def pool_copy(dst, src):
+            nc.gpsimd.tensor_scalar(dst, src, 1.0, 0.0, op0=ALU.mult, op1=ALU.add)
 
         def weave(i):
             n = steps[i][2]
-            woven[i] = ring.tile([P, 4 * n], BF16, name="woven", tag="woven%d" % (i % 2), align_bytes=64)
-            nc.scalar.copy(woven[i][:].bitcast(U32).rearrange("p (n u) -> p n u", u=2),
-                           gathered[i][:].rearrange("p (u n) -> p n u", u=2))
+            tag = "woven" if n == LONG else "woven%d" % (i % 2)
+            woven[i] = ring.tile([P, 4 * n], BF16, name="woven", tag=tag, align_bytes=64)
+            cut = GPSIMD_FROM if i in gpsimd_steps else n
+            nc.scalar.copy(woven[i][:, 0:4 * cut].bitcast(U32).rearrange("p (n u) -> p n u", u=2),
+                           gathered[i][:].rearrange("p (u n) -> p n u", u=2)[:, 0:cut, :])
+            if cut < n:
+                pool_copy(woven[i][:, 4 * cut:].rearrange("p (n u e) -> p n u e", u=2, e=2),
+                          gathered[i][:].bitcast(BF16).rearrange("p (u n e) -> p n u e", u=2, e=2)[:, cut:, :, :])
 
         def quantize(i):
             a, s0, n = steps[i]
-            for j0, j1 in ((0, 512), (512, n)) if n == 768 else ((0, n),):
-                nc.vector.quantize_mx(out=codes[a][:, s0 + j0:s0 + j1].bitcast(FP8X4), scales=scales[a][:, s0 + j0:s0 + j1],
-                                      in_=woven[i][:, 4 * j0:4 * j1])
+            nc.vector.quantize_mx(out=codes[a][:, s0:s0 + n].bitcast(FP8X4), scales=scales[a][:, s0:s0 + n], in_=woven[i][:])
 
-        shared_woven = {}
-
-        def shared_weave(a):
-            shared_woven[a] = ring.tile([P, 4 * T], BF16, name="shared_woven", align_bytes=64)
-            c0 = 2 * plane_start(a, 0)
-            nc.scalar.copy(shared_woven[a][:].bitcast(U32).rearrange("p (t u) -> p t u", u=2),
-                           planes[:, c0:c0 + 4 * T].bitcast(U32).rearrange("p (u t) -> p t u", u=2))
-
-        def shared_quantize(a, t0, t1, dst):
-            nc.vector.quantize_mx(out=dst.bitcast(FP8X4), scales=scales[a][:, S + t0:S + t1], in_=shared_woven[a][:, 4 * t0:4 * t1])
-
-        rows_bf = [keep.tile([P, 2 * PIECE], BF16, name="rows_bf%d" % d) for d in range(4)]
+        single_rows = [keep.tile([P, 2 * PIECE], BF16, name="single_row%d" % d) for d in range(4)]
         for d in range(4):
-            nc.vector.memset(rows_bf[d][:, T:], 0.0)
+            nc.vector.memset(single_rows[d][:, T:], 0.0)
 
-        def cast_rows():
-            for d in range(2):
-                nc.scalar.copy(rows_bf[d][:, 0:T], raw[0, 0][:, d, :])
-                nc.gpsimd.tensor_scalar(rows_bf[2 + d][:, 0:T], raw[0, 1][:, d, :], 1.0, 0.0, op0=ALU.mult, op1=ALU.add)
+        def make_single_rows():
+            c0 = plane_column(0, 0)
+            pairs = planes[:, c0:c0 + 2 * T].rearrange("p (t e) -> p e t", e=2)
+            for e in range(2):
+                pool_copy(single_rows[e][:, 0:T], pairs[:, e, :])
+            for e in range(2):
+                pool_copy(single_rows[2 + e][:, 0:T], raw[0, 1][:, e, :])
 
-        scalar_woven = {}
-
+        pieces = range(SCALAR_FROM, S, PIECE)
         staged = {}
-        pieces = [(s0, min(PIECE, S - s0)) for s0 in range(SCALAR_FROM, S, PIECE)]
+        piece_woven = {}
 
-        def scalar_gather(j, rows):
-            s0, n = pieces[j]
-            if j not in staged:
-                staged[j] = ring.tile([P, 4 * n], BF16, name="staged", tag="staged%d" % (j % 2))
-            idx = offs_sb[:, s0 // 16:(s0 + n) // 16]
-            for d in rows:
-                nc.scalar.activation(staged[j][:, d * n:(d + 1) * n], rows_bf[d][:].indirect(idx), ACT.Copy)
+        def piece_gather(j, d):
+            idx = offs_sb[:, pieces[j] // 16:(pieces[j] + PIECE) // 16]
+            nc.scalar.activation(staged[j][:, d * PIECE:(d + 1) * PIECE], single_rows[d][:].indirect(idx), ACT.Copy)
 
-        def scalar_weave(j):
-            scalar_woven[j] = ring.tile([P, 4 * pieces[j][1]], BF16, name="scalar_woven", align_bytes=64)
-            nc.scalar.copy(scalar_woven[j][:].rearrange("p (c i d) -> p c d i", i=4, d=4),
+        def piece_begin(j):
+            staged[j] = ring.tile([P, 4 * PIECE], BF16, name="staged", tag="staged%d" % (j % 2))
+            for d in range(3):
+                piece_gather(j, d)
+
+        def piece_finish(j):
+            piece_gather(j, 3)
+            piece_woven[j] = ring.tile([P, 4 * PIECE], BF16, name="piece_woven", align_bytes=64)
+            nc.scalar.copy(piece_woven[j][:].rearrange("p (c i d) -> p c d i", i=4, d=4),
                            staged[j][:].rearrange("p (d c i) -> p c d i", d=4, i=4))
 
-        def scalar_quantize(j):
-            s0, n = pieces[j]
-            nc.vector.quantize_mx(out=codes[0][:, s0:s0 + n].bitcast(FP8X4), scales=scales[0][:, s0:s0 + n], in_=scalar_woven[j][:])
+        def piece_quantize(j):
+            cols = slice(pieces[j], pieces[j] + PIECE)
+            nc.vector.quantize_mx(out=codes[0][:, cols].bitcast(FP8X4), scales=scales[0][:, cols], in_=piece_woven[j][:])
 
         def product(acc, e, a, rhs, rhs_scale):
             g = e * PASSES + a
@@ -220,60 +228,62 @@ def tile_moe_shr_lin_silu_kernel(tc, xT, w_words, w_scales, b, gate, offs, pos1,
             a, s0, n = steps[i]
             return range(s0 // C, (s0 + n) // C) if a == PASSES - 1 else ()
 
-        def shared_quantize_whole(a):
-            shared_quantize(a, 0, 512, shared_codes[a][:, 0:512])
-            shared_quantize(a, 512, T, shared_codes[a][:, 512:T])
-
-        casts_at = {0: [(1, 0), (1, 1)], 2: [(2, 0), (2, 1)], 3: [(3, 0)], 4: [(3, 1)]}
-        begun_at = {1: 0, 4: 1, 6: 2}
-        pieces_at = {3: 0, 5: 1, 7: 2}
-        shared_at = {1: 0, 5: 1, 7: 2, 9: 3}
         shared_groups = ((0, 512), (512, P), (512 + P, P))
         shared_sums = [psum.tile([P, n], F32, name="shared_sums", tag="bank%d" % (4 + j)) for j, (t0, n) in enumerate(shared_groups)]
+        shared_woven = {}
+
+        def shared_weave(a):
+            shared_woven[a] = ring.tile([P, 4 * T], BF16, name="shared_woven", align_bytes=64)
+            c0 = plane_column(a, 0)
+            nc.scalar.copy(shared_woven[a][:].bitcast(U32).rearrange("p (t u) -> p t u", u=2),
+                           planes[:, c0:c0 + 4 * T].bitcast(U32).rearrange("p (u t) -> p t u", u=2))
+
+        def shared_quantize(a, t0, t1, dst):
+            nc.vector.quantize_mx(out=dst.bitcast(FP8X4), scales=scales[a][:, S + t0:S + t1], in_=shared_woven[a][:, 4 * t0:4 * t1])
 
         def shared_products(a, operands):
             for j, (t0, n) in enumerate(shared_groups):
                 product(shared_sums[j][:], E, a, operands[j], scales[a][:, S + t0:S + t0 + n])
 
-        last = len(steps) - 1
+        round_plane(nc.scalar.copy, 1, 0, 0, T)
+        round_plane(nc.scalar.copy, 1, 1, 0, T)
+        make_single_rows()
         for i in range(len(steps)):
             gather(i)
+            if i >= 1:
+                quantize(i - 1)
             weave(i)
-            if i - 1 in shared_at and shared_at[i - 1] < 3:
-                a = shared_at[i - 1]
-                shared_quantize_whole(a)
+            if i % 2 == 0 and 0 <= i // 2 - 2 < len(pieces):
+                piece_quantize(i // 2 - 2)
+            if i % 2 == 1 and 0 <= i // 2 - 1 < PASSES - 1:
+                a = i // 2 - 1
+                shared_quantize(a, 0, 512, shared_codes[a][:, 0:512])
+                shared_quantize(a, 512, T, shared_codes[a][:, 512:T])
                 shared_products(a, [shared_codes[a][:, t0:t0 + n] for t0, n in shared_groups])
-            for a, u in casts_at.get(i, ()):
-                cast("s", a, u, 0, T)
-            if i == 1:
-                cast_rows()
-            if i in pieces_at:
-                scalar_gather(pieces_at[i], (3,))
-                scalar_weave(pieces_at[i])
-            if i in shared_at:
-                shared_weave(shared_at[i])
-            if i in begun_at:
-                scalar_gather(begun_at[i], (0, 1, 2))
+            if i < 4:
+                round_plane(nc.scalar.copy, 2 + i // 2, i % 2, 0, T)
+            if i % 2 == 0 and 0 <= i // 2 - 1 < PASSES:
+                shared_weave(i // 2 - 1)
+            if i < 2 * len(pieces):
+                (piece_finish if i % 2 else piece_begin)(i // 2)
             if i >= 2:
                 for e in experts_of(i - 2):
                     expert_silu(e)
             if i >= 1:
-                quantize(i - 1)
                 for e in experts_of(i - 1):
                     expert_products(e)
-            if i - 1 in pieces_at:
-                scalar_quantize(pieces_at[i - 1])
+
         late_a = ring.tile([P, 512], U32, name="late_a", tag="woven%d" % ((last - 1) % 2), align_bytes=64)
-        shared_quantize(3, 0, 512, late_a[:])
+        shared_quantize(PASSES - 1, 0, 512, late_a[:])
         for e in experts_of(last - 1):
             expert_silu(e)
         quantize(last)
         for e in experts_of(last):
             expert_products(e)
             expert_silu(e)
-        late_b = ring.tile([P, 256], U32, name="late_b", tag="woven%d" % (last % 2), align_bytes=64)
-        shared_quantize(3, 512, T, late_b[:])
-        shared_products(3, [late_a[:], late_b[:, 0:P], late_b[:, P:2 * P]])
+        late_b = ring.tile([P, T - 512], U32, name="late_b", tag="woven%d" % (last % 2), align_bytes=64)
+        shared_quantize(PASSES - 1, 512, T, late_b[:])
+        shared_products(PASSES - 1, [late_a[:], late_b[:, 0:P], late_b[:, P:2 * P]])
         for j, (t0, n) in enumerate(shared_groups):
             nc.scalar.activation(ys[:, t0:t0 + n], shared_sums[j][:], ACT.Silu, bias=bias[:, E:E + 1])
 
@@ -290,17 +300,17 @@ def tile_moe_shr_lin_silu_kernel(tc, xT, w_words, w_scales, b, gate, offs, pos1,
                     nc.tensor.transpose(turned[:, j * P:(j + 1) * P], picked[:, j * P:(j + 1) * P], ident[:])
                 gated = tail.tile([P, HALF], F32, name="gated")
                 for j in range(BLOCKS):
-                    col = 6 * r + h * BLOCKS + j
+                    col = gate_column[r] + h * BLOCKS + j
                     nc.scalar.activation(gated[:, j * P:(j + 1) * P], turned[:, j * P:(j + 1) * P], ACT.Copy,
                                          scale=gate_cols[:, col:col + 1])
                 for j in range(BLOCKS):
-                    nc.tensor.matmul(sums[j][:], gated[:, j * P:(j + 1) * P], ident[:], start=(r == 0), stop=(r == turned_terms - 1),
-                                     is_transpose=True)
+                    nc.tensor.matmul(sums[j][:], gated[:, j * P:(j + 1) * P], ident[:], start=(r == 0),
+                                     stop=(r == turned_terms - 1), is_transpose=True)
             rest = ys[:, h * HALF:(h + 1) * HALF]
             for r in range(turned_terms, TOP):
                 direct = tail.tile([P, HALF], F32, name="picked")
-                nc.vector.tensor_tensor(direct[:], y[:].indirect(pos_sb[r][:, HALF // 16:]), gate_rest[r][:], ALU.mult)
-                added = tail.tile([P, HALF], F32, name="added", bufs=2)
+                nc.vector.tensor_tensor(direct[:], y[:].indirect(pos_sb[r][:, HALF // 16:]), gate_direct[r][:], ALU.mult)
+                added = tail.tile([P, HALF], F32, name="added", bufs=DIRECT)
                 nc.vector.tensor_tensor(added[:], direct[:], rest, ALU.add)
                 rest = added[:]
             result = tail.tile([P, HALF], F32, name="result", bufs=2)

from contextlib import ExitStack

import concourse.mybir as mybir
from concourse.masks import make_identity

K, T, E, C, N = 2048, 768, 12, 256, 128
TOP = 4
S = E * C
FLOPS = 2 * K * N * (S + T)

F32 = mybir.dt.float32
BF16 = mybir.dt.bfloat16
I32 = mybir.dt.int32
U32 = mybir.dt.uint32
U16 = mybir.dt.uint16
U8 = mybir.dt.uint8
FP8X4 = mybir.dt.float8_e4m3fn_x4
FP4X4 = mybir.dt.float4_e2m1fn_x4
ACT = mybir.ActivationFunctionType
ALU = mybir.AluOpType

P = 128
PASSES = K // 512
LONG = 1024
NARROW = 512
PIECE = 512
SCALAR_FROM = LONG
GPSIMD_FROM = 640
FIRST_CAST_SPLIT = 512
HALF = T // 2
BLOCKS = HALF // P
DIRECT = 2


def tile_moe_shr_lin_silu_kernel(tc, xT, w_words, w_scales, b, gate, offs, pos1, pos2, pos3, pos4, out):
    nc = tc.nc
    with ExitStack() as ctx:
        lists = ctx.enter_context(tc.tile_pool(name="lists", bufs=1))
        keep = ctx.enter_context(tc.tile_pool(name="keep", bufs=1))
        raws = ctx.enter_context(tc.tile_pool(name="raws", bufs=4))
        ring = ctx.enter_context(tc.tile_pool(name="ring", bufs=1))
        tail = ctx.enter_context(tc.tile_pool(name="tail", bufs=TOP))
        psum = ctx.enter_context(tc.psum_pool(name="psum", bufs=1))

        raw = {}

        def load_rows(a, u):
            raw[a, u] = raws.tile([P, 2, T], F32, name="raw")
            rows = xT[512 * a:512 * (a + 1), :].rearrange("(p u e) t -> p u e t", u=2, e=2)
            nc.sync.dma_start(raw[a, u][:], rows[:, u, :, :])

        load_rows(0, 0)
        offs_sb = lists.tile([P, S // 16], U16, name="offs_sb")
        nc.sync.dma_start(offs_sb[:], offs)
        load_rows(0, 1)
        load_rows(1, 0)
        load_rows(1, 1)

        planes = keep.tile([P, 2 * PASSES * T * 2], BF16, name="planes", align_bytes=64)

        def plane_column(a, u):
            return 2 * T * (2 * (PASSES - 1 - a) + u)

        def round_plane(copy, a, u, t0, t1):
            c0 = plane_column(a, u)
            copy(planes[:, c0 + 2 * t0:c0 + 2 * t1].rearrange("p (t e) -> p t e", e=2),
                 raw[a, u][:, :, t0:t1].rearrange("p e t -> p t e"))

        w_scale_sb = keep.tile([P, (E + 1) * PASSES * N], U8, name="w_scale_sb", align_bytes=64)
        nc.vector.memset(w_scale_sb[:].bitcast(I32), 0)
        gate_rows = keep.tile([P, P], F32, name="gate_rows")
        nc.vector.memset(gate_rows[:], 0.0)
        ident = keep.tile([P, P], F32, name="ident")
        make_identity(nc, ident[:])

        warm = keep.tile([P, 1], F32, name="warm")
        nc.scalar.activation(warm[:], gate_rows[:, 0:1], ACT.Silu)
        round_plane(nc.vector.tensor_copy, 0, 0, 0, FIRST_CAST_SPLIT)
        round_plane(nc.scalar.copy, 0, 0, FIRST_CAST_SPLIT, T)
        round_plane(nc.scalar.copy, 0, 1, 0, T)

        for u in range(2):
            load_rows(2, u)
        matrices = (E + 1) * PASSES
        w_sb = keep.tile([P, matrices * 2 * N], U8, name="w_sb", align_bytes=64)
        w_dst = w_sb[:].bitcast(I32).rearrange("p (g c) -> p g c", c=2 * N // 4)
        w_src = w_words.rearrange("e a p c -> p (e a) c").bitcast(I32)
        first_six = 6 * PASSES
        for g0, g1 in ((0, first_six), (first_six, matrices)):
            nc.sync.dma_start(w_dst[:, g0:g1, :], w_src[:, g0:g1, :])
        for u in range(2):
            load_rows(3, u)
        s_src = w_scales.rearrange("e a q n -> q (e a) n").bitcast(I32)
        for quadrant in range(4):
            s_dst = w_scale_sb[32 * quadrant:32 * quadrant + 4, :].bitcast(I32).rearrange("p (g c) -> p g c", c=N // 4)
            nc.sync.dma_start(s_dst, s_src[4 * quadrant:4 * quadrant + 4, :, :])
        bias = keep.tile([P, E + 1], F32, name="bias")
        nc.sync.dma_start(bias[:], b)
        pos_sb = []
        for r, pos in enumerate((pos1, pos2, pos3, pos4)):
            pos_sb.append(lists.tile([P, T // 16], U16, name="pos_sb%d" % r))
            nc.sync.dma_start(pos_sb[r][:], pos)

        gate_column = {}
        gate_blocks = 0
        for r in range(TOP):
            blocks = 2 * BLOCKS if r < TOP - DIRECT else BLOCKS
            nc.sync.dma_start(gate_rows[gate_blocks:gate_blocks + blocks, :],
                              gate[r, 0, 0:blocks * P].rearrange("(j t) -> j t", t=P))
            gate_column[r] = gate_blocks
            gate_blocks = gate_blocks + blocks
        gate_direct = {}
        for r in range(TOP - DIRECT, TOP):
            gate_direct[r] = keep.tile([P, HALF], F32, name="gate_direct%d" % r)
            nc.sync.dma_start(gate_direct[r][:], gate[r, :, HALF:])
        gate_ps = psum.tile([P, P], F32, name="gate_ps", tag="bank7")
        nc.tensor.transpose(gate_ps[:], gate_rows[:], ident[:])
        gate_cols = keep.tile([P, gate_blocks], F32, name="gate_cols")
        nc.scalar.copy(gate_cols[:], gate_ps[:, 0:gate_blocks])

        codes = [keep.tile([P, S], U32, name="codes%d" % a, align_bytes=64) for a in range(PASSES)]
        scales = [keep.tile([P, S + T], U8, name="scales%d" % a, align_bytes=64) for a in range(PASSES)]
        shared_codes = [keep.tile([P, T], U32, name="shared_codes%d" % a, align_bytes=64) for a in range(PASSES - 1)]
        y = keep.tile([P, S], F32, name="y")
        ys = keep.tile([P, T], F32, name="ys")

        steps = [(0, 0, SCALAR_FROM)] + [(1, s0, LONG) for s0 in range(0, S, LONG)]
        steps += [(a, s0, LONG) for s0 in range(0, S - LONG, LONG) for a in (2, 3)]
        steps += [(2, S - LONG, LONG), (3, S - LONG, 2 * C), (3, S - 2 * C, C), (3, S - C, C)]
        last = len(steps) - 1
        gpsimd_steps = [i for i in range(last) if steps[i + 1][2] == LONG]

        gathered = {}
        woven = {}

        def gather(i):
            a, s0, n = steps[i]
            gathered[i] = ring.tile([P, 2 * n], U32, name="gathered", tag="gathered%d" % (i % 2))
            for u in range(2):
                count = min(n, NARROW if a == 0 or (i, u) == (1, 0) else LONG)
                words = T if count <= NARROW else 2 * T
                c0 = plane_column(a, u)
                window = planes[:, c0:c0 + 2 * words].bitcast(U32)
                for j in range(0, n, count):
                    idx = offs_sb[:, (s0 + j) // 16:(s0 + j + count) // 16]
                    nc.vector.tensor_copy(gathered[i][:, u * n + j:u * n + j + count], window.indirect(idx))

        def pool_copy(dst, src):
            nc.gpsimd.tensor_scalar(dst, src, 1.0, 0.0, op0=ALU.mult, op1=ALU.add)

        def weave(i):
            n = steps[i][2]
            tag = "woven" if n == LONG else "woven%d" % (i % 2)
            woven[i] = ring.tile([P, 4 * n], BF16, name="woven", tag=tag, align_bytes=64)
            cut = GPSIMD_FROM if i in gpsimd_steps else n
            nc.scalar.copy(woven[i][:, 0:4 * cut].bitcast(U32).rearrange("p (n u) -> p n u", u=2),
                           gathered[i][:].rearrange("p (u n) -> p n u", u=2)[:, 0:cut, :])
            if cut < n:
                pool_copy(woven[i][:, 4 * cut:].rearrange("p (n u e) -> p n u e", u=2, e=2),
                          gathered[i][:].bitcast(BF16).rearrange("p (u n e) -> p n u e", u=2, e=2)[:, cut:, :, :])

        def quantize(i):
            a, s0, n = steps[i]
            nc.vector.quantize_mx(out=codes[a][:, s0:s0 + n].bitcast(FP8X4), scales=scales[a][:, s0:s0 + n], in_=woven[i][:])

        single_rows = [keep.tile([P, 2 * PIECE], BF16, name="single_row%d" % d) for d in range(4)]
        for d in range(4):
            nc.vector.memset(single_rows[d][:, T:], 0.0)

        def make_single_rows():
            c0 = plane_column(0, 0)
            pairs = planes[:, c0:c0 + 2 * T].rearrange("p (t e) -> p e t", e=2)
            for e in range(2):
                pool_copy(single_rows[e][:, 0:T], pairs[:, e, :])
            for e in range(2):
                pool_copy(single_rows[2 + e][:, 0:T], raw[0, 1][:, e, :])

        pieces = range(SCALAR_FROM, S, PIECE)
        staged = {}
        piece_woven = {}

        def piece_gather(j, d):
            idx = offs_sb[:, pieces[j] // 16:(pieces[j] + PIECE) // 16]
            nc.scalar.activation(staged[j][:, d * PIECE:(d + 1) * PIECE], single_rows[d][:].indirect(idx), ACT.Copy)

        def piece_begin(j):
            staged[j] = ring.tile([P, 4 * PIECE], BF16, name="staged", tag="staged%d" % (j % 2))
            for d in range(3):
                piece_gather(j, d)

        def piece_finish(j):
            piece_gather(j, 3)
            piece_woven[j] = ring.tile([P, 4 * PIECE], BF16, name="piece_woven", align_bytes=64)
            nc.scalar.copy(piece_woven[j][:].rearrange("p (c i d) -> p c d i", i=4, d=4),
                           staged[j][:].rearrange("p (d c i) -> p c d i", d=4, i=4))

        def piece_quantize(j):
            cols = slice(pieces[j], pieces[j] + PIECE)
            nc.vector.quantize_mx(out=codes[0][:, cols].bitcast(FP8X4), scales=scales[0][:, cols], in_=piece_woven[j][:])

        def product(acc, e, a, rhs, rhs_scale):
            g = e * PASSES + a
            nc.tensor.matmul_mx(out=acc, lhsT=w_sb[:, g * 2 * N:(g + 1) * 2 * N].bitcast(FP4X4),
                                lhsT_scale=w_scale_sb[:, g * N:(g + 1) * N],
                                rhs=rhs.bitcast(FP8X4), rhs_scale=rhs_scale,
                                start=(a == 0), stop=(a == PASSES - 1))

        sums_of = {}

        def expert_products(e):
            if e < E - 1:
                acc = psum.tile([P, C], F32, name="acc", tag="bank%d" % (e % 4))
                sums_of[e] = [(acc[:], e * C, C)]
                order = [(acc[:, h * P:(h + 1) * P], h, a) for h in range(2) for a in range(PASSES)]
            else:
                accs = [psum.tile([P, P], F32, name="acc_last", tag="bank%d" % (3 + 4 * h)) for h in range(2)]
                sums_of[e] = [(accs[h][:], e * C + h * P, P) for h in range(2)]
                order = [(accs[h][:], h, a) for a in range(PASSES) for h in range(2)]
            for dst, h, a in order:
                cols = slice(e * C + h * P, e * C + (h + 1) * P)
                product(dst, e, a, codes[a][:, cols], scales[a][:, cols])

        def expert_silu(e):
            for acc, c0, n in sums_of[e]:
                nc.scalar.activation(y[:, c0:c0 + n], acc, ACT.Silu, bias=bias[:, e:e + 1])

        def experts_of(i):
            a, s0, n = steps[i]
            return range(s0 // C, (s0 + n) // C) if a == PASSES - 1 else ()

        shared_groups = ((0, 512), (512, P), (512 + P, P))
        shared_sums = [psum.tile([P, n], F32, name="shared_sums", tag="bank%d" % (4 + j)) for j, (t0, n) in enumerate(shared_groups)]
        shared_woven = {}

        def shared_weave(a):
            shared_woven[a] = ring.tile([P, 4 * T], BF16, name="shared_woven", align_bytes=64)
            c0 = plane_column(a, 0)
            nc.scalar.copy(shared_woven[a][:].bitcast(U32).rearrange("p (t u) -> p t u", u=2),
                           planes[:, c0:c0 + 4 * T].bitcast(U32).rearrange("p (u t) -> p t u", u=2))

        def shared_quantize(a, t0, t1, dst):
            nc.vector.quantize_mx(out=dst.bitcast(FP8X4), scales=scales[a][:, S + t0:S + t1], in_=shared_woven[a][:, 4 * t0:4 * t1])

        def shared_products(a, operands):
            for j, (t0, n) in enumerate(shared_groups):
                product(shared_sums[j][:], E, a, operands[j], scales[a][:, S + t0:S + t0 + n])

        round_plane(nc.scalar.copy, 1, 0, 0, T)
        round_plane(nc.scalar.copy, 1, 1, 0, T)
        make_single_rows()
        for i in range(len(steps)):
            gather(i)
            if i >= 1:
                quantize(i - 1)
            weave(i)
            if i % 2 == 0 and 0 <= i // 2 - 2 < len(pieces):
                piece_quantize(i // 2 - 2)
            if i % 2 == 1 and 0 <= i // 2 - 1 < PASSES - 1:
                a = i // 2 - 1
                shared_quantize(a, 0, 512, shared_codes[a][:, 0:512])
                shared_quantize(a, 512, T, shared_codes[a][:, 512:T])
                shared_products(a, [shared_codes[a][:, t0:t0 + n] for t0, n in shared_groups])
            if i < 4:
                round_plane(nc.scalar.copy, 2 + i // 2, i % 2, 0, T)
            if i % 2 == 0 and 0 <= i // 2 - 1 < PASSES:
                shared_weave(i // 2 - 1)
            if i < 2 * len(pieces):
                (piece_finish if i % 2 else piece_begin)(i // 2)
            if i >= 2:
                for e in experts_of(i - 2):
                    expert_silu(e)
            if i >= 1:
                for e in experts_of(i - 1):
                    expert_products(e)

        late_a = ring.tile([P, 512], U32, name="late_a", tag="woven%d" % ((last - 1) % 2), align_bytes=64)
        shared_quantize(PASSES - 1, 0, 512, late_a[:])
        for e in experts_of(last - 1):
            expert_silu(e)
        quantize(last)
        for e in experts_of(last):
            expert_products(e)
            expert_silu(e)
        late_b = ring.tile([P, T - 512], U32, name="late_b", tag="woven%d" % (last % 2), align_bytes=64)
        shared_quantize(PASSES - 1, 512, T, late_b[:])
        shared_products(PASSES - 1, [late_a[:], late_b[:, 0:P], late_b[:, P:2 * P]])
        for j, (t0, n) in enumerate(shared_groups):
            nc.scalar.activation(ys[:, t0:t0 + n], shared_sums[j][:], ACT.Silu, bias=bias[:, E:E + 1])

        sum_banks = (2, 3, 7, 4, 5, 6)
        for h in range(2):
            turned_terms = TOP - DIRECT * h
            sums = [psum.tile([P, P], F32, name="sums", tag="bank%d" % sum_banks[h * BLOCKS + j]) for j in range(BLOCKS)]
            for r in range(turned_terms):
                picked = tail.tile([P, HALF], F32, name="picked")
                idx = pos_sb[r][:, h * HALF // 16:(h + 1) * HALF // 16]
                nc.vector.tensor_copy(picked[:], y[:].indirect(idx))
                turned = psum.tile([P, HALF], F32, name="turned", tag="bank%d" % (r % 2))
                for j in range(BLOCKS):
                    nc.tensor.transpose(turned[:, j * P:(j + 1) * P], picked[:, j * P:(j + 1) * P], ident[:])
                gated = tail.tile([P, HALF], F32, name="gated")
                for j in range(BLOCKS):
                    col = gate_column[r] + h * BLOCKS + j
                    nc.scalar.activation(gated[:, j * P:(j + 1) * P], turned[:, j * P:(j + 1) * P], ACT.Copy,
                                         scale=gate_cols[:, col:col + 1])
                for j in range(BLOCKS):
                    nc.tensor.matmul(sums[j][:], gated[:, j * P:(j + 1) * P], ident[:], start=(r == 0),
                                     stop=(r == turned_terms - 1), is_transpose=True)
            rest = ys[:, h * HALF:(h + 1) * HALF]
            for r in range(turned_terms, TOP):
                direct = tail.tile([P, HALF], F32, name="picked")
                nc.vector.tensor_tensor(direct[:], y[:].indirect(pos_sb[r][:, HALF // 16:]), gate_direct[r][:], ALU.mult)
                added = tail.tile([P, HALF], F32, name="added", bufs=DIRECT)
                nc.vector.tensor_tensor(added[:], direct[:], rest, ALU.add)
                rest = added[:]
            result = tail.tile([P, HALF], F32, name="result", bufs=2)
            for j in range(BLOCKS):
                t0 = h * HALF + j * P
                nc.vector.tensor_tensor(result[:, j * P:(j + 1) * P], sums[j][:], rest[:, j * P:(j + 1) * P], ALU.add)
                nc.sync.dma_start(out[:, t0:t0 + P], result[:, j * P:(j + 1) * P])
